import numpy as np
import ml_dtypes


def mxq(x, axis, fmt="e4m3"):
    dtype, down = {"e4m3": (ml_dtypes.float8_e4m3fn, 7), "e5m2": (ml_dtypes.float8_e5m2, 14)}[fmt]
    v = np.moveaxis(np.asarray(x, np.float32).astype(ml_dtypes.bfloat16).astype(np.float64), axis, -1)
    blocks = v.reshape(v.shape[:-1] + (-1, 32))
    amax = np.abs(blocks).max(-1, keepdims=True)
    byte = np.maximum(np.where(amax > 0, np.frexp(amax)[1] - 1 + 127, 0) - down, 1)
    scale = np.exp2(byte - 127.0)
    codes = (blocks / scale).astype(np.float32).astype(dtype).astype(np.float64)
    return np.moveaxis((codes * scale).reshape(v.shape), -1, axis)


WIDE = False


def mx_kscale(k):
    if not WIDE:
        return np.ones(k)
    levels = np.array([10, -10, 5, -5, 0])
    if k % 512:
        return np.exp2(np.random.permutation(np.resize(levels, k // 32))).repeat(32)
    a = np.empty((k // 512, 16))
    for p in range(k // 512):
        a[p, :8] = np.random.permutation(np.resize(levels, 8))
        for g in range(8):
            far = levels[np.abs(levels - a[p, g]) >= 10]
            a[p, g + 8] = far[np.random.randint(len(far))]
    return np.exp2(a.ravel()).repeat(32)


def f64(x):
    return np.asarray(x).astype(np.float64)


def striped(idx):
    return np.tile(idx.reshape(-1, 16).T, (8, 1)).astype(np.uint16)


def unstriped(offs):
    return offs[:16].T.reshape(-1).astype(np.int64)


def striped8(idx):
    return np.concatenate([x.reshape(-1, 16).T for x in idx]).astype(np.uint16)


def runs(offs, k):
    lists = np.stack([offs[16 * r : 16 * r + 16].T.reshape(-1) for r in range(8)]).astype(np.int64)
    return lists[np.arange(k) % 512 // 64]


def pack_weight(w):
    k, n = w.shape
    w = f64(np.asarray(w, np.float32).astype(ml_dtypes.bfloat16)).reshape(k // 32, 32, n)
    amax = np.abs(w).max(1)
    byte = np.clip(np.where(amax > 0, np.frexp(amax)[1] - 1 + 127 - 7, 1), 1, 254)
    scaled = (w * np.exp2(127.0 - byte)[:, None, :]).reshape(k, n).astype(np.float32)
    words = np.ascontiguousarray(scaled.reshape(k // 512, 128, 4, n).transpose(0, 1, 3, 2)).astype(ml_dtypes.float8_e4m3fn).view(np.uint8)
    return words, np.ascontiguousarray(byte.astype(np.uint8).reshape(k // 512, 16, n))


def unpack_weight(words, scales):
    g, p, n, _ = words.shape
    vals = np.ascontiguousarray(words).view(ml_dtypes.float8_e4m3fn).astype(np.float64) * np.repeat(np.exp2(scales.astype(np.float64) - 127.0), 8, axis=1)[..., None]
    return vals.transpose(0, 1, 3, 2).reshape(g * 512, n)

def planes(y):
    n, m = y.shape
    v = y.astype(np.float32).astype(ml_dtypes.bfloat16).astype(np.float64).reshape(n // 32, 32, m)
    top = np.abs(v).max(1)
    byte = np.clip(np.where(top > 0, np.frexp(top)[1] - 1 + 127 - 7, 1), 1, 254)
    codes = (v * np.exp2(127.0 - byte)[:, None, :]).reshape(n, m).astype(np.float32).astype(ml_dtypes.float8_e4m3fn).view(np.uint8)
    words = codes.reshape(n // 512, 128, 4, m).transpose(0, 1, 3, 2)
    return np.ascontiguousarray(words), np.ascontiguousarray(byte.astype(np.uint8).reshape(n // 512, 16, m))


K, T, S, N, H = 512, 2048, 512, 512, 512


def setup_inputs():
    n = np.random.standard_normal
    s = mx_kscale(K)[:, None]
    u = mx_kscale(H)
    packed_xT = pack_weight(n((K, T)) * s)
    packed_w1 = pack_weight(n((K, H)) / np.sqrt(K) / s)
    packed_w2 = pack_weight(n((K, H)) / np.sqrt(K) / s)
    packed_w3 = pack_weight(n((H, N)) / np.sqrt(H) / u[:, None])
    return {
        "x_words": packed_xT[0],
        "x_scales": packed_xT[1],
        "w1_words": packed_w1[0],
        "w1_scales": packed_w1[1],
        "w2_words": packed_w2[0],
        "w2_scales": packed_w2[1],
        "gn": (np.random.uniform(0.5, 1.5, (H, 1)) * u[:, None]).astype(np.float32),
        "w3_words": packed_w3[0],
        "w3_scales": packed_w3[1],
        "offs": striped(np.random.permutation(T)[:S]),
        "hz": striped8(np.random.randint(0, T, (8, S))),
        "n1": striped(np.random.permutation(S)),
        "n2": striped(np.random.permutation(S)),
        "n3": striped(np.random.permutation(S)),
    }


def reference(x_words, x_scales, w1_words, w1_scales, w2_words, w2_scales, gn, w3_words, w3_scales, offs, hz, n1, n2, n3):
    xq = unpack_weight(x_words, x_scales)[:, unstriped(offs)]
    y = unpack_weight(w1_words, w1_scales).T @ xq
    x_hz = unpack_weight(x_words, x_scales)[np.arange(K)[:, None], runs(hz, K)]
    d = unpack_weight(w2_words, w2_scales).T @ x_hz
    z = f64(gn) * (y * (np.tanh(d[:, unstriped(n1)] - d[:, unstriped(n2)])))
    h = unpack_weight(w3_words, w3_scales).T @ mxq(z, 0, "e4m3")
    st = h - h[:, unstriped(n3)]
    out_0 = st - (0.5 * st[:, unstriped(n3)])
    return (out_0,) + planes(out_0)

@@ -1,0 +1,266 @@
+from contextlib import ExitStack
+
+import concourse.mybir as mybir
+
+F32 = mybir.dt.float32
+BF16 = mybir.dt.bfloat16
+I32 = mybir.dt.int32
+U32 = mybir.dt.uint32
+U16 = mybir.dt.uint16
+U8 = mybir.dt.uint8
+FP8X4 = mybir.dt.float8_e4m3fn_x4
+ALU = mybir.AluOpType
+ACT = mybir.ActivationFunctionType
+
+P = 128
+T = 2048
+S = 512
+PACK = 4
+HALF = 256
+CHUNKS = [slice(0, 256), slice(256, 384), slice(384, 512)]
+FLOPS = 3 * 2 * 512 * 512 * 512
+
+
+def tile_picked_twhjointbtwice_none_po_kernel(
+    tc, x_words, x_scales, w1_words, w1_scales, w2_words, w2_scales, gn, w3_words, w3_scales,
+    offs, hz, n1, n2, n3, out_0, out_1, out_2,
+):
+    nc = tc.nc
+    with ExitStack() as ctx:
+        lists = ctx.enter_context(tc.tile_pool(name="lists", bufs=1))
+        keep = ctx.enter_context(tc.tile_pool(name="keep", bufs=1))
+        ring = ctx.enter_context(tc.tile_pool(name="ring", bufs=3))
+        psum = ctx.enter_context(tc.psum_pool(name="psum", bufs=1))
+
+        def sb(name, shape, dtype, tag=""):
+            return keep.tile(shape, dtype, name=name, tag=tag or name, align_bytes=64)
+
+        def load_list(name, src):
+            tile = lists.tile([P, S // 16], U16, name=name)
+            nc.sync.dma_start(tile[:], src)
+            return tile
+
+        def load_words(name, src, width):
+            tile = sb(name, [P, width], I32)
+            nc.sync.dma_start(tile[:], src[0].rearrange("p n r -> p (n r)").bitcast(I32))
+            return tile
+
+        def load_scale_rows(queue, tile, src, first):
+            for q in range(4):
+                queue.dma_start(
+                    tile[32 * q + first : 32 * q + first + 4, :].bitcast(I32),
+                    src[0, 4 * q : 4 * q + 4, :].bitcast(I32),
+                )
+
+        def deal_words(engine, name, raw):
+            dealt = sb(name, [P, PACK, P], I32)
+            engine.tensor_copy(
+                dealt[:].rearrange("p t (c i) -> p c t i", i=4),
+                raw[:].rearrange("p (c i t) -> p c t i", i=4, t=PACK),
+            )
+            return dealt
+
+        def deal_bytes(engine, name, raw, tag=""):
+            dealt = sb(name, [P, PACK, P], U8, tag)
+            engine.tensor_copy(dealt[:], raw[:].rearrange("p (m t) -> p t m", t=PACK))
+            return dealt
+
+        def gather_scales(name, window, offsets):
+            picked = sb(name, [P, S], U8)
+            nc.vector.tensor_copy(picked[:], window[:].indirect(offsets[:]))
+            return picked
+
+        def place_scales(queue, plane, picked):
+            for r in range(4):
+                queue.dma_start(plane[r:P:32, :].bitcast(I32), picked[8 * r : P : 32, :].bitcast(I32))
+
+        def zeroed(name):
+            tile = sb(name, [P, S], U8)
+            nc.vector.memset(tile[:].bitcast(I32), 0)
+            return tile
+
+        def gather_words(name, window, offsets):
+            picked = sb(name, [P, S], U32)
+            nc.vector.tensor_copy(picked[:], window[:].bitcast(U32).indirect(offsets[:]))
+            return picked
+
+        def product(out, w, w_scale, first, t, rhs, rhs_scale):
+            nc.tensor.matmul_mx(
+                out=out, lhsT=w[:, t, :].bitcast(FP8X4), lhsT_scale=w_scale[first:P, t, :],
+                rhs=rhs.bitcast(FP8X4), rhs_scale=rhs_scale, start=True, stop=True,
+            )
+
+        def interleave(dst, src):
+            nc.vector.tensor_copy(
+                dst[:].rearrange("p (c i) t -> p c t i", i=4),
+                src[:].rearrange("p t (c i) -> p c t i", i=4),
+            )
+
+        def part(offsets, cols):
+            return offsets[:, cols.start // 16 : cols.stop // 16]
+
+        xs = sb("xs", [P, T], U8)
+        nc.vector.memset(xs[:].bitcast(I32), 0)
+        w2s_raw = zeroed("w2s_raw")
+        w1s_raw = zeroed("w1s_raw")
+        w3s_raw = zeroed("w3s_raw")
+        hz_plane = zeroed("hz_plane")
+        offs_plane = zeroed("offs_plane")
+
+        hz_t = load_list("hz_t", hz)
+        offs_t = load_list("offs_t", offs)
+        nc.sync.dma_start(xs[0:P:8, :].bitcast(I32), x_scales[0].bitcast(I32))
+        xw = load_words("xw", x_words, T)
+        load_scale_rows(nc.scalar, w2s_raw, w2_scales, 0)
+        load_scale_rows(nc.gpsimd, w1s_raw, w1_scales, 0)
+        gain = sb("gain", [P, PACK], F32)
+        nc.gpsimd.dma_start(gain[:], gn.rearrange("(p t) o -> p (t o)", t=PACK))
+        w2_raw = load_words("w2_raw", w2_words, S)
+
+        hz_picked = gather_scales("hz_picked", xs, hz_t)
+        place_scales(nc.sync, hz_plane, hz_picked)
+        offs_picked = gather_scales("offs_picked", xs, offs_t)
+        hz_words = gather_words("hz_words", xw, hz_t)
+        offs_words = gather_words("offs_words", xw, offs_t)
+        w2s = deal_bytes(nc.gpsimd, "w2s", w2s_raw)
+        w2 = deal_words(nc.gpsimd, "w2", w2_raw)
+
+        n2_t = load_list("n2_t", n2)
+        n1_t = load_list("n1_t", n1)
+        w1_raw = load_words("w1_raw", w1_words, S)
+        place_scales(nc.sync, offs_plane, offs_picked)
+        w3_raw = load_words("w3_raw", w3_words, S)
+        load_scale_rows(nc.sync, w3s_raw, w3_scales, 0)
+        n3_t = load_list("n3_t", n3)
+        w1s = deal_bytes(nc.gpsimd, "w1s", w1s_raw, tag="w2_raw")
+        w1 = deal_words(nc.gpsimd, "w1", w1_raw)
+        w3 = deal_words(nc.vector, "w3", w3_raw)
+        w3s = deal_bytes(nc.vector, "w3s", w3s_raw)
+
+        d_ps = [psum.tile([P, S], F32, name=f"d_ps{t}", tag=f"bank{t}") for t in range(PACK)]
+        y_ps = [psum.tile([P, S], F32, name=f"y_ps{t}", tag=f"bank{PACK + t}") for t in range(PACK)]
+        for t in range(PACK):
+            product(d_ps[t][:], w2, w2s, 0, t, hz_words[:], hz_plane[:])
+        for t in range(PACK):
+            product(y_ps[t][:], w1, w1s, 0, t, offs_words[:], offs_plane[:])
+
+        d = [sb(f"d{t}", [P, S], F32) for t in range(PACK)]
+        h_sb = [sb(f"h{t}", [P, S], F32) for t in range(PACK)]
+        h_ps = [psum.tile([P, S], F32, name=f"h_ps{t}", tag=f"bank{t}") for t in range(PACK)]
+        units = [(c, t) for c in range(len(CHUNKS)) for t in range(PACK)]
+        width = [cols.stop - cols.start for cols in CHUNKS]
+        diff, gate = {}, {}
+        z_rows = [sb(f"z_rows{c}", [P, PACK, w], BF16) for c, w in enumerate(width)]
+        z_grouped = [sb(f"z_grouped{c}", [P, w, PACK], BF16) for c, w in enumerate(width)]
+
+        early = slice(0, CHUNKS[-1].start)
+
+        def fetch(u):
+            c, t = units[u]
+            if c == 0 and t in (2, 3):
+                nc.vector.tensor_copy(d[t][:], d_ps[t][:])
+            elif c == 0:
+                nc.scalar.activation(d[t][:], d_ps[t][:], ACT.Copy)
+            second = ring.tile([P, width[c]], F32, name="second", align_bytes=64)
+            diff[u] = ring.tile([P, width[c]], F32, name="diff", align_bytes=64)
+            nc.scalar.activation(second[:], d[t][:].indirect(part(n2_t, CHUNKS[c])), ACT.Copy)
+            nc.vector.tensor_tensor(diff[u][:], d[t][:].indirect(part(n1_t, CHUNKS[c])), second[:], ALU.subtract)
+
+        def squash(u):
+            gate[u] = ring.tile([P, width[units[u][0]]], F32, name="gate", align_bytes=64)
+            nc.scalar.activation(gate[u][:], diff[u][:], ACT.Tanh)
+
+        def scale(u):
+            c, t = units[u]
+            nc.vector.scalar_tensor_tensor(
+                z_rows[c][:, t, :], y_ps[t][:, CHUNKS[c]], gain[:, t : t + 1], gate[u][:], ALU.mult, ALU.mult
+            )
+
+        def group(u):
+            c, t = units[u]
+            if t == PACK - 1:
+                interleave(z_grouped[c], z_rows[c])
+
+        def project(u):
+            c, t = units[u]
+            if t == PACK - 1:
+                z_words = sb(f"z_words{c}", [P, width[c]], U32)
+                z_plane = sb(f"z_plane{c}", [P, width[c]], U8)
+                nc.vector.quantize_mx(
+                    out=z_words[:].bitcast(FP8X4), scales=z_plane[:],
+                    in_=z_grouped[c][:].rearrange("p j t -> p (j t)"),
+                )
+                for m in range(PACK):
+                    if u == len(units) - 1:
+                        nc.scalar.activation(h_sb[m][:, early], h_ps[m][:, early], ACT.Copy)
+                    product(h_ps[m][:, CHUNKS[c]], w3, w3s, 0, m, z_words[:], z_plane[:])
+
+        stages = [fetch, squash, scale, group, project]
+        for step in range(len(units) + len(stages) - 1):
+            for lag, stage in enumerate(stages):
+                if 0 <= step - lag < len(units):
+                    stage(step - lag)
+
+
+        halves = [slice(0, HALF), slice(HALF, S)]
+        st = [sb(f"st{t}", [P, S], F32) for t in range(PACK)]
+        near = [sb(f"near{t}", [P, S], F32) for t in range(PACK)]
+        last = CHUNKS[-1]
+        for t in (1, 0, 2, 3):
+            if t == 1:
+                nc.vector.tensor_copy(h_sb[t][:, last], h_ps[t][:, last])
+            else:
+                nc.scalar.activation(h_sb[t][:, last], h_ps[t][:, last], ACT.Copy)
+            for cols in halves:
+                if t == 1:
+                    nc.vector.tensor_copy(near[t][:, cols], h_sb[t][:].indirect(part(n3_t, cols)))
+                else:
+                    nc.scalar.activation(near[t][:, cols], h_sb[t][:].indirect(part(n3_t, cols)), ACT.Copy)
+        res = [sb(f"res{c}", [P, PACK, w], F32) for c, w in enumerate(width)]
+        out_rows = out_0.rearrange("(p t) j -> p t j", t=PACK)
+        minus_half = sb("minus_half", [P, S], F32)
+        for t in (1, 0, 2, 3):
+            nc.vector.tensor_tensor(st[t][:], h_ps[t][:], near[t][:], ALU.subtract)
+            if t == 0:
+                nc.vector.tensor_scalar(minus_half[:], st[1][:], -0.5, None, ALU.mult)
+                for c, cols in enumerate(CHUNKS):
+                    nc.vector.tensor_tensor(res[c][:, 1, :], minus_half[:].indirect(part(n3_t, cols)), st[1][:, cols], ALU.add)
+                nc.sync.dma_start(out_rows[:, 1, CHUNKS[0]], res[0][:, 1, :])
+
+        o_words = sb("o_words", [P, S], U32)
+        o_plane = sb("o_plane", [P, S], U8)
+        words_out = out_1[0].rearrange("p n r -> p (n r)").bitcast(I32)
+        o_grouped = [sb(f"o_grouped{c}", [P, w, PACK], BF16) for c, w in enumerate(width)]
+        units2 = [(c, t) for c in range(len(CHUNKS)) for t in (0, 2, 3)]
+
+        def finish(u):
+            c, t = units2[u]
+            far = ring.tile([P, width[c]], F32, name="far", align_bytes=64)
+            nc.scalar.activation(far[:], st[t][:].indirect(part(n3_t, CHUNKS[c])), ACT.Copy)
+            nc.vector.scalar_tensor_tensor(res[c][:, t, :], far[:], -0.5, st[t][:, CHUNKS[c]], ALU.mult, ALU.add)
+            if c == 0:
+                nc.sync.dma_start(out_rows[:, t, CHUNKS[c]], res[c][:, t, :])
+            elif t == PACK - 1:
+                nc.sync.dma_start(out_rows[:, :, CHUNKS[c]], res[c][:])
+
+        def regroup(u):
+            c, t = units2[u]
+            if t == PACK - 1:
+                interleave(o_grouped[c], res[c])
+
+        def pack(u):
+            c, t = units2[u]
+            if t == PACK - 1:
+                nc.vector.quantize_mx(
+                    out=o_words[:, CHUNKS[c]].bitcast(FP8X4), scales=o_plane[:, CHUNKS[c]],
+                    in_=o_grouped[c][:].rearrange("p j t -> p (j t)"),
+                )
+                nc.sync.dma_start(words_out[:, CHUNKS[c]], o_words[:, CHUNKS[c]].bitcast(I32))
+
+        stages2 = [finish, regroup, pack]
+        for step in range(len(units2) + len(stages2) - 1):
+            for lag, stage in enumerate(stages2):
+                if 0 <= step - lag < len(units2):
+                    stage(step - lag)
+        for q in range(4):
+            (nc.sync if q == 3 else nc.scalar).dma_start(out_2[0, 4 * q : 4 * q + 4, :].bitcast(I32), o_plane[32 * q : 32 * q + 4, :].bitcast(I32))

@@ -18,6 +18,7 @@ S = 512
 PACK = 4
 HALF = 256
 CHUNKS = [slice(0, 256), slice(256, 384), slice(384, 512)]
+OCHUNKS = [slice(0, 256), slice(256, 512)]
 FLOPS = 3 * 2 * 512 * 512 * 512
 
 
@@ -74,9 +75,9 @@ def tile_picked_twhjointbtwice_none_po_kernel(
             for r in range(4):
                 queue.dma_start(plane[r:P:32, :].bitcast(I32), picked[8 * r : P : 32, :].bitcast(I32))
 
-        def zeroed(name):
-            tile = sb(name, [P, S], U8)
-            nc.vector.memset(tile[:].bitcast(I32), 0)
+        def zeroed(engine, name, width):
+            tile = sb(name, [P, width], U8)
+            engine.memset(tile[:].bitcast(I32), 0)
             return tile
 
         def gather_words(name, window, offsets):
@@ -90,31 +91,35 @@ def tile_picked_twhjointbtwice_none_po_kernel(
                 rhs=rhs.bitcast(FP8X4), rhs_scale=rhs_scale, start=True, stop=True,
             )
 
-        def interleave(dst, src):
-            nc.vector.tensor_copy(
+        def interleave(copy, dst, src):
+            copy(
                 dst[:].rearrange("p (c i) t -> p c t i", i=4),
                 src[:].rearrange("p t (c i) -> p c t i", i=4),
             )
+
+        def move(on_vector, out, in_):
+            if on_vector:
+                nc.vector.tensor_copy(out, in_)
+            else:
+                nc.scalar.activation(out, in_, ACT.Copy)
 
         def part(offsets, cols):
             return offsets[:, cols.start // 16 : cols.stop // 16]
 
         xs = sb("xs", [P, T], U8)
-        nc.vector.memset(xs[:].bitcast(I32), 0)
-        w2s_raw = zeroed("w2s_raw")
-        w1s_raw = zeroed("w1s_raw")
-        w3s_raw = zeroed("w3s_raw")
-        hz_plane = zeroed("hz_plane")
-        offs_plane = zeroed("offs_plane")
+        nc.gpsimd.memset(xs[:, : T // 2].bitcast(I32), 0)
+        nc.vector.memset(xs[:, T // 2 :].bitcast(I32), 0)
+        w2s_raw = zeroed(nc.gpsimd, "w2s_raw", S)
+        hz_plane = zeroed(nc.vector, "hz_plane", S)
+        w1s_raw = zeroed(nc.vector, "w1s_raw", S)
+        offs_plane = zeroed(nc.vector, "offs_plane", S)
+        w3s_raw = zeroed(nc.vector, "w3s_raw", S)
 
         hz_t = load_list("hz_t", hz)
         offs_t = load_list("offs_t", offs)
         nc.sync.dma_start(xs[0:P:8, :].bitcast(I32), x_scales[0].bitcast(I32))
         xw = load_words("xw", x_words, T)
         load_scale_rows(nc.scalar, w2s_raw, w2_scales, 0)
-        load_scale_rows(nc.gpsimd, w1s_raw, w1_scales, 0)
-        gain = sb("gain", [P, PACK], F32)
-        nc.gpsimd.dma_start(gain[:], gn.rearrange("(p t) o -> p (t o)", t=PACK))
         w2_raw = load_words("w2_raw", w2_words, S)
 
         hz_picked = gather_scales("hz_picked", xs, hz_t)
@@ -125,15 +130,18 @@ def tile_picked_twhjointbtwice_none_po_kernel(
         w2s = deal_bytes(nc.gpsimd, "w2s", w2s_raw)
         w2 = deal_words(nc.gpsimd, "w2", w2_raw)
 
-        n2_t = load_list("n2_t", n2)
-        n1_t = load_list("n1_t", n1)
         w1_raw = load_words("w1_raw", w1_words, S)
+        load_scale_rows(nc.sync, w1s_raw, w1_scales, 0)
+        n2_t = load_list("n2_t", n2)
         place_scales(nc.sync, offs_plane, offs_picked)
+        gain = sb("gain", [P, PACK], F32)
+        nc.sync.dma_start(gain[:], gn.rearrange("(p t) o -> p (t o)", t=PACK))
+        n1_t = load_list("n1_t", n1)
         w3_raw = load_words("w3_raw", w3_words, S)
         load_scale_rows(nc.sync, w3s_raw, w3_scales, 0)
         n3_t = load_list("n3_t", n3)
-        w1s = deal_bytes(nc.gpsimd, "w1s", w1s_raw, tag="w2_raw")
         w1 = deal_words(nc.gpsimd, "w1", w1_raw)
+        w1s = deal_bytes(nc.gpsimd, "w1s", w1s_raw)
         w3 = deal_words(nc.vector, "w3", w3_raw)
         w3s = deal_bytes(nc.vector, "w3s", w3s_raw)
 
@@ -157,17 +165,15 @@ def tile_picked_twhjointbtwice_none_po_kernel(
 
         def fetch(u):
             c, t = units[u]
-            if c == 0 and t in (2, 3):
-                nc.vector.tensor_copy(d[t][:], d_ps[t][:])
-            elif c == 0:
-                nc.scalar.activation(d[t][:], d_ps[t][:], ACT.Copy)
-            second = ring.tile([P, width[c]], F32, name="second", align_bytes=64)
-            diff[u] = ring.tile([P, width[c]], F32, name="diff", align_bytes=64)
-            nc.scalar.activation(second[:], d[t][:].indirect(part(n2_t, CHUNKS[c])), ACT.Copy)
+            if c == 0:
+                move(t in (1, 2, 3), d[t][:], d_ps[t][:])
+            second = ring.tile([P, width[c]], F32, name="second", align_bytes=64, bufs=4)
+            diff[u] = ring.tile([P, width[c]], F32, name="diff", align_bytes=64, bufs=4)
+            move(u in (), second[:], d[t][:].indirect(part(n2_t, CHUNKS[c])))
             nc.vector.tensor_tensor(diff[u][:], d[t][:].indirect(part(n1_t, CHUNKS[c])), second[:], ALU.subtract)
 
         def squash(u):
-            gate[u] = ring.tile([P, width[units[u][0]]], F32, name="gate", align_bytes=64)
+            gate[u] = ring.tile([P, width[units[u][0]]], F32, name="gate", align_bytes=64, bufs=4)
             nc.scalar.activation(gate[u][:], diff[u][:], ACT.Tanh)
 
         def scale(u):
@@ -179,7 +185,7 @@ def tile_picked_twhjointbtwice_none_po_kernel(
         def group(u):
             c, t = units[u]
             if t == PACK - 1:
-                interleave(z_grouped[c], z_rows[c])
+                interleave(nc.scalar.copy if c in (0,) else nc.vector.tensor_copy, z_grouped[c], z_rows[c])
 
         def project(u):
             c, t = units[u]
@@ -192,7 +198,7 @@ def tile_picked_twhjointbtwice_none_po_kernel(
                 )
                 for m in range(PACK):
                     if u == len(units) - 1:
-                        nc.scalar.activation(h_sb[m][:, early], h_ps[m][:, early], ACT.Copy)
+                        move(m in (), h_sb[m][:, early], h_ps[m][:, early])
                     product(h_ps[m][:, CHUNKS[c]], w3, w3s, 0, m, z_words[:], z_plane[:])
 
         stages = [fetch, squash, scale, group, project]
@@ -206,56 +212,52 @@ def tile_picked_twhjointbtwice_none_po_kernel(
         st = [sb(f"st{t}", [P, S], F32) for t in range(PACK)]
         near = [sb(f"near{t}", [P, S], F32) for t in range(PACK)]
         last = CHUNKS[-1]
-        for t in (1, 0, 2, 3):
-            if t == 1:
-                nc.vector.tensor_copy(h_sb[t][:, last], h_ps[t][:, last])
-            else:
-                nc.scalar.activation(h_sb[t][:, last], h_ps[t][:, last], ACT.Copy)
-            for cols in halves:
-                if t == 1:
-                    nc.vector.tensor_copy(near[t][:, cols], h_sb[t][:].indirect(part(n3_t, cols)))
-                else:
-                    nc.scalar.activation(near[t][:, cols], h_sb[t][:].indirect(part(n3_t, cols)), ACT.Copy)
-        res = [sb(f"res{c}", [P, PACK, w], F32) for c, w in enumerate(width)]
+        for t in range(PACK):
+            move(t in (0, 2), h_sb[t][:, last], h_ps[t][:, last])
+            for i, cols in enumerate(halves):
+                move(t in (0, 2) or (t, i) in (0, 2), near[t][:, cols], h_sb[t][:].indirect(part(n3_t, cols)))
+        owidth = [cols.stop - cols.start for cols in OCHUNKS]
+        res = [sb(f"res{c}", [P, PACK, w], F32) for c, w in enumerate(owidth)]
         out_rows = out_0.rearrange("(p t) j -> p t j", t=PACK)
-        minus_half = sb("minus_half", [P, S], F32)
-        for t in (1, 0, 2, 3):
+        minus_half = {}
+        for t in (0, 1, 2, 3):
             nc.vector.tensor_tensor(st[t][:], h_ps[t][:], near[t][:], ALU.subtract)
-            if t == 0:
-                nc.vector.tensor_scalar(minus_half[:], st[1][:], -0.5, None, ALU.mult)
-                for c, cols in enumerate(CHUNKS):
-                    nc.vector.tensor_tensor(res[c][:, 1, :], minus_half[:].indirect(part(n3_t, cols)), st[1][:, cols], ALU.add)
-                nc.sync.dma_start(out_rows[:, 1, CHUNKS[0]], res[0][:, 1, :])
+        for t in (0,):
+            minus_half[t] = sb(f"minus_half{t}", [P, S], F32)
+            nc.vector.tensor_scalar(minus_half[t][:], st[t][:], -0.5, None, ALU.mult)
 
         o_words = sb("o_words", [P, S], U32)
         o_plane = sb("o_plane", [P, S], U8)
         words_out = out_1[0].rearrange("p n r -> p (n r)").bitcast(I32)
-        o_grouped = [sb(f"o_grouped{c}", [P, w, PACK], BF16) for c, w in enumerate(width)]
-        units2 = [(c, t) for c in range(len(CHUNKS)) for t in (0, 2, 3)]
+        o_grouped = [sb(f"o_grouped{c}", [P, w, PACK], BF16) for c, w in enumerate(owidth)]
+        units2 = [(c, t) for c in range(len(OCHUNKS)) for t in (0, 1, 2, 3)]
 
         def finish(u):
             c, t = units2[u]
-            far = ring.tile([P, width[c]], F32, name="far", align_bytes=64)
-            nc.scalar.activation(far[:], st[t][:].indirect(part(n3_t, CHUNKS[c])), ACT.Copy)
-            nc.vector.scalar_tensor_tensor(res[c][:, t, :], far[:], -0.5, st[t][:, CHUNKS[c]], ALU.mult, ALU.add)
-            if c == 0:
-                nc.sync.dma_start(out_rows[:, t, CHUNKS[c]], res[c][:, t, :])
-            elif t == PACK - 1:
-                nc.sync.dma_start(out_rows[:, :, CHUNKS[c]], res[c][:])
+            cols = OCHUNKS[c]
+            if t in (0,):
+                nc.vector.tensor_tensor(res[c][:, t, :], minus_half[t][:].indirect(part(n3_t, cols)), st[t][:, cols], ALU.add)
+            else:
+                far = ring.tile([P, owidth[c]], F32, name="far", align_bytes=64, bufs=4)
+                move((c, t) in (), far[:], st[t][:].indirect(part(n3_t, cols)))
+                nc.vector.scalar_tensor_tensor(res[c][:, t, :], far[:], -0.5, st[t][:, cols], ALU.mult, ALU.add)
+            if t == (0, 1, 2, 3)[-1]:
+                nc.sync.dma_start(out_rows[:, :, cols], res[c][:])
 
         def regroup(u):
             c, t = units2[u]
-            if t == PACK - 1:
-                interleave(o_grouped[c], res[c])
+            if t == (0, 1, 2, 3)[-1]:
+                interleave(nc.scalar.copy if c in (0,) else nc.vector.tensor_copy, o_grouped[c], res[c])
 
         def pack(u):
             c, t = units2[u]
-            if t == PACK - 1:
+            cols = OCHUNKS[c]
+            if t == (0, 1, 2, 3)[-1]:
                 nc.vector.quantize_mx(
-                    out=o_words[:, CHUNKS[c]].bitcast(FP8X4), scales=o_plane[:, CHUNKS[c]],
+                    out=o_words[:, cols].bitcast(FP8X4), scales=o_plane[:, cols],
                     in_=o_grouped[c][:].rearrange("p j t -> p (j t)"),
                 )
-                nc.sync.dma_start(words_out[:, CHUNKS[c]], o_words[:, CHUNKS[c]].bitcast(I32))
+                nc.sync.dma_start(words_out[:, cols], o_words[:, cols].bitcast(I32))
 
         stages2 = [finish, regroup, pack]
         for step in range(len(units2) + len(stages2) - 1):

@@ -17,7 +17,7 @@ T = 2048
 S = 512
 PACK = 4
 HALF = 256
-CHUNKS = [slice(0, 256), slice(256, 384), slice(384, 512)]
+CHUNKS = [slice(0, 256), slice(256, 512)]
 OCHUNKS = [slice(0, 256), slice(256, 512)]
 FLOPS = 3 * 2 * 512 * 512 * 512
 
@@ -53,11 +53,11 @@ def tile_picked_twhjointbtwice_none_po_kernel(
                     src[0, 4 * q : 4 * q + 4, :].bitcast(I32),
                 )
 
-        def deal_words(engine, name, raw):
-            dealt = sb(name, [P, PACK, P], I32)
-            engine.tensor_copy(
+        def deal_words(copy, name, raw):
+            dealt = sb(name, [P, PACK, P], U32)
+            copy(
                 dealt[:].rearrange("p t (c i) -> p c t i", i=4),
-                raw[:].rearrange("p (c i t) -> p c t i", i=4, t=PACK),
+                raw[:].bitcast(U32).rearrange("p (c i t) -> p c t i", i=4, t=PACK),
             )
             return dealt
 
@@ -106,44 +106,41 @@ def tile_picked_twhjointbtwice_none_po_kernel(
         def part(offsets, cols):
             return offsets[:, cols.start // 16 : cols.stop // 16]
 
-        xs = sb("xs", [P, T], U8)
-        nc.gpsimd.memset(xs[:, : T // 2].bitcast(I32), 0)
-        nc.vector.memset(xs[:, T // 2 :].bitcast(I32), 0)
-        w2s_raw = zeroed(nc.gpsimd, "w2s_raw", S)
+        w2s_raw = zeroed(nc.vector, "w2s_raw", S)
+        xs = zeroed(nc.vector, "xs", T)
         hz_plane = zeroed(nc.vector, "hz_plane", S)
-        w1s_raw = zeroed(nc.vector, "w1s_raw", S)
+        w13s_raw = zeroed(nc.vector, "w13s_raw", S)
         offs_plane = zeroed(nc.vector, "offs_plane", S)
-        w3s_raw = zeroed(nc.vector, "w3s_raw", S)
 
         hz_t = load_list("hz_t", hz)
-        offs_t = load_list("offs_t", offs)
+        n2_t = load_list("n2_t", n2)
         nc.sync.dma_start(xs[0:P:8, :].bitcast(I32), x_scales[0].bitcast(I32))
         xw = load_words("xw", x_words, T)
         load_scale_rows(nc.scalar, w2s_raw, w2_scales, 0)
+        offs_t = load_list("offs_t", offs)
         w2_raw = load_words("w2_raw", w2_words, S)
 
         hz_picked = gather_scales("hz_picked", xs, hz_t)
         place_scales(nc.sync, hz_plane, hz_picked)
-        offs_picked = gather_scales("offs_picked", xs, offs_t)
+        w2s = deal_bytes(nc.vector, "w2s", w2s_raw)
         hz_words = gather_words("hz_words", xw, hz_t)
+        offs_picked = gather_scales("offs_picked", xs, offs_t)
         offs_words = gather_words("offs_words", xw, offs_t)
-        w2s = deal_bytes(nc.gpsimd, "w2s", w2s_raw)
-        w2 = deal_words(nc.gpsimd, "w2", w2_raw)
+        w2 = deal_words(nc.scalar.copy, "w2", w2_raw)
 
         w1_raw = load_words("w1_raw", w1_words, S)
-        load_scale_rows(nc.sync, w1s_raw, w1_scales, 0)
-        n2_t = load_list("n2_t", n2)
-        place_scales(nc.sync, offs_plane, offs_picked)
+        load_scale_rows(nc.sync, w13s_raw, w1_scales, 0)
+        load_scale_rows(nc.sync, w13s_raw, w3_scales, 4)
         gain = sb("gain", [P, PACK], F32)
         nc.sync.dma_start(gain[:], gn.rearrange("(p t) o -> p (t o)", t=PACK))
+        place_scales(nc.sync, offs_plane, offs_picked)
         n1_t = load_list("n1_t", n1)
         w3_raw = load_words("w3_raw", w3_words, S)
-        load_scale_rows(nc.sync, w3s_raw, w3_scales, 0)
         n3_t = load_list("n3_t", n3)
-        w1 = deal_words(nc.gpsimd, "w1", w1_raw)
-        w1s = deal_bytes(nc.gpsimd, "w1s", w1s_raw)
-        w3 = deal_words(nc.vector, "w3", w3_raw)
-        w3s = deal_bytes(nc.vector, "w3s", w3s_raw)
+        w1 = deal_words(nc.scalar.copy, "w1", w1_raw)
+        w1s = deal_bytes(nc.vector, "w13s", w13s_raw)
+        w3s = w1s
+        w3 = deal_words(nc.vector.tensor_copy, "w3", w3_raw)
 
         d_ps = [psum.tile([P, S], F32, name=f"d_ps{t}", tag=f"bank{t}") for t in range(PACK)]
         y_ps = [psum.tile([P, S], F32, name=f"y_ps{t}", tag=f"bank{PACK + t}") for t in range(PACK)]
@@ -161,12 +158,10 @@ def tile_picked_twhjointbtwice_none_po_kernel(
         z_rows = [sb(f"z_rows{c}", [P, PACK, w], BF16) for c, w in enumerate(width)]
         z_grouped = [sb(f"z_grouped{c}", [P, w, PACK], BF16) for c, w in enumerate(width)]
 
-        early = slice(0, CHUNKS[-1].start)
-
         def fetch(u):
             c, t = units[u]
             if c == 0:
-                move(t in (1, 2, 3), d[t][:], d_ps[t][:])
+                move(t in (2, 3), d[t][:], d_ps[t][:])
             second = ring.tile([P, width[c]], F32, name="second", align_bytes=64, bufs=4)
             diff[u] = ring.tile([P, width[c]], F32, name="diff", align_bytes=64, bufs=4)
             move(u in (), second[:], d[t][:].indirect(part(n2_t, CHUNKS[c])))
@@ -197,9 +192,9 @@ def tile_picked_twhjointbtwice_none_po_kernel(
                     in_=z_grouped[c][:].rearrange("p j t -> p (j t)"),
                 )
                 for m in range(PACK):
-                    if u == len(units) - 1:
-                        move(m in (), h_sb[m][:, early], h_ps[m][:, early])
-                    product(h_ps[m][:, CHUNKS[c]], w3, w3s, 0, m, z_words[:], z_plane[:])
+                    if c in {1: slice(0, 256)}:
+                        move(m in (), h_sb[m][:, {1: slice(0, 256)}[c]], h_ps[m][:, {1: slice(0, 256)}[c]])
+                    product(h_ps[m][:, CHUNKS[c]], w3, w3s, 4, m, z_words[:], z_plane[:])
 
         stages = [fetch, squash, scale, group, project]
         for step in range(len(units) + len(stages) - 1):
@@ -211,7 +206,7 @@ def tile_picked_twhjointbtwice_none_po_kernel(
         halves = [slice(0, HALF), slice(HALF, S)]
         st = [sb(f"st{t}", [P, S], F32) for t in range(PACK)]
         near = [sb(f"near{t}", [P, S], F32) for t in range(PACK)]
-        last = CHUNKS[-1]
+        last = slice(256, 512)
         for t in range(PACK):
             move(t in (0, 2), h_sb[t][:, last], h_ps[t][:, last])
             for i, cols in enumerate(halves):
@@ -241,8 +236,8 @@ def tile_picked_twhjointbtwice_none_po_kernel(
                 far = ring.tile([P, owidth[c]], F32, name="far", align_bytes=64, bufs=4)
                 move((c, t) in (), far[:], st[t][:].indirect(part(n3_t, cols)))
                 nc.vector.scalar_tensor_tensor(res[c][:, t, :], far[:], -0.5, st[t][:, cols], ALU.mult, ALU.add)
-            if t == (0, 1, 2, 3)[-1]:
-                nc.sync.dma_start(out_rows[:, :, cols], res[c][:])
+            if t % 2 == 2 - 1:
+                nc.sync.dma_start(out_rows[:, t + 1 - 2 : t + 1, cols], res[c][:, t + 1 - 2 : t + 1, :])
 
         def regroup(u):
             c, t = units2[u]

@@ -16,10 +16,13 @@ P = 128
 T = 2048
 S = 512
 PACK = 4
-HALF = 256
-CHUNKS = [slice(0, 256), slice(256, 512)]
-OCHUNKS = [slice(0, 256), slice(256, 512)]
-FLOPS = 3 * 2 * 512 * 512 * 512
+HALF = S // 2
+HALVES = [slice(0, HALF), slice(HALF, S)]
+RING = 4
+
+FUSED_TILE = 0
+
+FLOPS = 3 * 2 * S * S * S
 
 
 def tile_picked_twhjointbtwice_none_po_kernel(
@@ -30,11 +33,19 @@ def tile_picked_twhjointbtwice_none_po_kernel(
     with ExitStack() as ctx:
         lists = ctx.enter_context(tc.tile_pool(name="lists", bufs=1))
         keep = ctx.enter_context(tc.tile_pool(name="keep", bufs=1))
-        ring = ctx.enter_context(tc.tile_pool(name="ring", bufs=3))
+        ring = ctx.enter_context(tc.tile_pool(name="ring", bufs=RING))
         psum = ctx.enter_context(tc.psum_pool(name="psum", bufs=1))
 
-        def sb(name, shape, dtype, tag=""):
-            return keep.tile(shape, dtype, name=name, tag=tag or name, align_bytes=64)
+        def sb(name, shape, dtype):
+            return keep.tile(shape, dtype, name=name, align_bytes=64)
+
+        def passing(name):
+            return ring.tile([P, HALF], F32, name=name, align_bytes=64)
+
+        def zeroed(name, width):
+            tile = sb(name, [P, width], U8)
+            nc.vector.memset(tile[:].bitcast(I32), 0)
+            return tile
 
         def load_list(name, src):
             tile = lists.tile([P, S // 16], U16, name=name)
@@ -46,12 +57,10 @@ def tile_picked_twhjointbtwice_none_po_kernel(
             nc.sync.dma_start(tile[:], src[0].rearrange("p n r -> p (n r)").bitcast(I32))
             return tile
 
-        def load_scale_rows(queue, tile, src, first):
+        def load_plane(plane, src):
             for q in range(4):
-                queue.dma_start(
-                    tile[32 * q + first : 32 * q + first + 4, :].bitcast(I32),
-                    src[0, 4 * q : 4 * q + 4, :].bitcast(I32),
-                )
+                rows = slice(32 * q, 32 * q + PACK)
+                nc.sync.dma_start(plane[rows, :].bitcast(I32), src[0, PACK * q : PACK * (q + 1), :].bitcast(I32))
 
         def deal_words(copy, name, raw):
             dealt = sb(name, [P, PACK, P], U32)
@@ -61,40 +70,24 @@ def tile_picked_twhjointbtwice_none_po_kernel(
             )
             return dealt
 
-        def deal_bytes(engine, name, raw, tag=""):
-            dealt = sb(name, [P, PACK, P], U8, tag)
-            engine.tensor_copy(dealt[:], raw[:].rearrange("p (m t) -> p t m", t=PACK))
+        def deal_plane(name, raw):
+            dealt = sb(name, [P, PACK, P], U8)
+            nc.vector.tensor_copy(dealt[:], raw[:].rearrange("p (m t) -> p t m", t=PACK))
             return dealt
 
-        def gather_scales(name, window, offsets):
-            picked = sb(name, [P, S], U8)
-            nc.vector.tensor_copy(picked[:], window[:].indirect(offsets[:]))
+        def gather_packed(name, window, dtype, offsets):
+            picked = sb(name, [P, S], dtype)
+            nc.vector.tensor_copy(picked[:], window[:].bitcast(dtype).indirect(offsets[:]))
             return picked
 
-        def place_scales(queue, plane, picked):
-            for r in range(4):
-                queue.dma_start(plane[r:P:32, :].bitcast(I32), picked[8 * r : P : 32, :].bitcast(I32))
+        def place_rows(plane, picked):
+            for r in range(PACK):
+                nc.sync.dma_start(plane[r:P:32, :].bitcast(I32), picked[8 * r : P : 32, :].bitcast(I32))
 
-        def zeroed(engine, name, width):
-            tile = sb(name, [P, width], U8)
-            engine.memset(tile[:].bitcast(I32), 0)
-            return tile
-
-        def gather_words(name, window, offsets):
-            picked = sb(name, [P, S], U32)
-            nc.vector.tensor_copy(picked[:], window[:].bitcast(U32).indirect(offsets[:]))
-            return picked
-
-        def product(out, w, w_scale, first, t, rhs, rhs_scale):
+        def product(out, weights, weight_plane, t, words, plane):
             nc.tensor.matmul_mx(
-                out=out, lhsT=w[:, t, :].bitcast(FP8X4), lhsT_scale=w_scale[first:P, t, :],
-                rhs=rhs.bitcast(FP8X4), rhs_scale=rhs_scale, start=True, stop=True,
-            )
-
-        def interleave(copy, dst, src):
-            copy(
-                dst[:].rearrange("p (c i) t -> p c t i", i=4),
-                src[:].rearrange("p t (c i) -> p c t i", i=4),
+                out=out, lhsT=weights[:, t, :].bitcast(FP8X4), lhsT_scale=weight_plane[:, t, :],
+                rhs=words.bitcast(FP8X4), rhs_scale=plane, start=True, stop=True,
             )
 
         def move(on_vector, out, in_):
@@ -103,161 +96,155 @@ def tile_picked_twhjointbtwice_none_po_kernel(
             else:
                 nc.scalar.activation(out, in_, ACT.Copy)
 
-        def part(offsets, cols):
-            return offsets[:, cols.start // 16 : cols.stop // 16]
+        def look_up(window, offsets, half):
+            return window[:].indirect(offsets[:, half * HALF // 16 : (half + 1) * HALF // 16])
 
-        w2s_raw = zeroed(nc.vector, "w2s_raw", S)
-        xs = zeroed(nc.vector, "xs", T)
-        hz_plane = zeroed(nc.vector, "hz_plane", S)
-        w13s_raw = zeroed(nc.vector, "w13s_raw", S)
-        offs_plane = zeroed(nc.vector, "offs_plane", S)
+        def group(half, grouped, rows):
+            copy = nc.vector.tensor_copy if half else nc.scalar.copy
+            copy(grouped[:].rearrange("p (c i) t -> p c t i", i=4), rows[:].rearrange("p t (c i) -> p c t i", i=4))
 
-        hz_t = load_list("hz_t", hz)
-        n2_t = load_list("n2_t", n2)
-        nc.sync.dma_start(xs[0:P:8, :].bitcast(I32), x_scales[0].bitcast(I32))
-        xw = load_words("xw", x_words, T)
-        load_scale_rows(nc.scalar, w2s_raw, w2_scales, 0)
-        offs_t = load_list("offs_t", offs)
+        def quantise(words, plane, grouped):
+            nc.vector.quantize_mx(out=words.bitcast(FP8X4), scales=plane, in_=grouped[:].rearrange("p j t -> p (j t)"))
+
+        def pipeline(stages):
+            pieces = [(half, t) for half in range(2) for t in range(PACK)]
+            for step in range(len(pieces) + len(stages) - 1):
+                for lag, stage in enumerate(stages):
+                    if 0 <= step - lag < len(pieces):
+                        stage(*pieces[step - lag])
+
+        w2_plane_raw = zeroed("w2_plane_raw", S)
+        x_rows = zeroed("x_rows", T)
+        hz_plane = zeroed("hz_plane", S)
+        w1_plane_raw = zeroed("w1_plane_raw", S)
+        offs_plane = zeroed("offs_plane", S)
+
+        hz_list = load_list("hz_list", hz)
+        offs_list = load_list("offs_list", offs)
+        load_plane(w2_plane_raw, w2_scales)
+        nc.sync.dma_start(x_rows[0:P:8, :].bitcast(I32), x_scales[0].bitcast(I32))
+        x_table = load_words("x_table", x_words, T)
         w2_raw = load_words("w2_raw", w2_words, S)
 
-        hz_picked = gather_scales("hz_picked", xs, hz_t)
-        place_scales(nc.sync, hz_plane, hz_picked)
-        w2s = deal_bytes(nc.vector, "w2s", w2s_raw)
-        hz_words = gather_words("hz_words", xw, hz_t)
-        offs_picked = gather_scales("offs_picked", xs, offs_t)
-        offs_words = gather_words("offs_words", xw, offs_t)
+        w2_plane = deal_plane("w2_plane", w2_plane_raw)
+        hz_rows = gather_packed("hz_rows", x_rows, U8, hz_list)
+        place_rows(hz_plane, hz_rows)
+        hz_words = gather_packed("hz_words", x_table, U32, hz_list)
+        offs_rows = gather_packed("offs_rows", x_rows, U8, offs_list)
+        offs_words = gather_packed("offs_words", x_table, U32, offs_list)
         w2 = deal_words(nc.scalar.copy, "w2", w2_raw)
 
+        n2_list = load_list("n2_list", n2)
         w1_raw = load_words("w1_raw", w1_words, S)
-        load_scale_rows(nc.sync, w13s_raw, w1_scales, 0)
-        load_scale_rows(nc.sync, w13s_raw, w3_scales, 4)
+        load_plane(w1_plane_raw, w1_scales)
+        place_rows(offs_plane, offs_rows)
+        n1_list = load_list("n1_list", n1)
         gain = sb("gain", [P, PACK], F32)
         nc.sync.dma_start(gain[:], gn.rearrange("(p t) o -> p (t o)", t=PACK))
-        place_scales(nc.sync, offs_plane, offs_picked)
-        n1_t = load_list("n1_t", n1)
         w3_raw = load_words("w3_raw", w3_words, S)
-        n3_t = load_list("n3_t", n3)
+        w3_plane_raw = zeroed("w3_plane_raw", S)
+        load_plane(w3_plane_raw, w3_scales)
+        n3_list = load_list("n3_list", n3)
         w1 = deal_words(nc.scalar.copy, "w1", w1_raw)
-        w1s = deal_bytes(nc.vector, "w13s", w13s_raw)
-        w3s = w1s
+        w1_plane = deal_plane("w1_plane", w1_plane_raw)
+        w3_plane = deal_plane("w3_plane", w3_plane_raw)
         w3 = deal_words(nc.vector.tensor_copy, "w3", w3_raw)
 
-        d_ps = [psum.tile([P, S], F32, name=f"d_ps{t}", tag=f"bank{t}") for t in range(PACK)]
-        y_ps = [psum.tile([P, S], F32, name=f"y_ps{t}", tag=f"bank{PACK + t}") for t in range(PACK)]
+        d_psum = [psum.tile([P, S], F32, name=f"d_psum{t}", tag=f"bank{t}") for t in range(PACK)]
+        y_psum = [psum.tile([P, S], F32, name=f"y_psum{t}", tag=f"bank{PACK + t}") for t in range(PACK)]
         for t in range(PACK):
-            product(d_ps[t][:], w2, w2s, 0, t, hz_words[:], hz_plane[:])
+            product(d_psum[t][:], w2, w2_plane, t, hz_words[:], hz_plane[:])
         for t in range(PACK):
-            product(y_ps[t][:], w1, w1s, 0, t, offs_words[:], offs_plane[:])
+            product(y_psum[t][:], w1, w1_plane, t, offs_words[:], offs_plane[:])
 
         d = [sb(f"d{t}", [P, S], F32) for t in range(PACK)]
-        h_sb = [sb(f"h{t}", [P, S], F32) for t in range(PACK)]
-        h_ps = [psum.tile([P, S], F32, name=f"h_ps{t}", tag=f"bank{t}") for t in range(PACK)]
-        units = [(c, t) for c in range(len(CHUNKS)) for t in range(PACK)]
-        width = [cols.stop - cols.start for cols in CHUNKS]
-        diff, gate = {}, {}
-        z_rows = [sb(f"z_rows{c}", [P, PACK, w], BF16) for c, w in enumerate(width)]
-        z_grouped = [sb(f"z_grouped{c}", [P, w, PACK], BF16) for c, w in enumerate(width)]
+        h = [sb(f"h{t}", [P, S], F32) for t in range(PACK)]
+        h_psum = [psum.tile([P, S], F32, name=f"h_psum{t}", tag=f"bank{t}") for t in range(PACK)]
+        z_rows = [sb(f"z_rows{half}", [P, PACK, HALF], BF16) for half in range(2)]
+        z_grouped = [sb(f"z_grouped{half}", [P, HALF, PACK], BF16) for half in range(2)]
+        difference, gate = {}, {}
 
-        def fetch(u):
-            c, t = units[u]
-            if c == 0:
-                move(t in (2, 3), d[t][:], d_ps[t][:])
-            second = ring.tile([P, width[c]], F32, name="second", align_bytes=64, bufs=4)
-            diff[u] = ring.tile([P, width[c]], F32, name="diff", align_bytes=64, bufs=4)
-            move(u in (), second[:], d[t][:].indirect(part(n2_t, CHUNKS[c])))
-            nc.vector.tensor_tensor(diff[u][:], d[t][:].indirect(part(n1_t, CHUNKS[c])), second[:], ALU.subtract)
+        def subtract_d(half, t):
+            if half == 0:
+                move(t > 0, d[t][:], d_psum[t][:])
+            d_at_n2 = passing("d_at_n2")
+            difference[half, t] = passing("difference")
+            move(False, d_at_n2[:], look_up(d[t], n2_list, half))
+            nc.vector.tensor_tensor(difference[half, t][:], look_up(d[t], n1_list, half), d_at_n2[:], ALU.subtract)
 
-        def squash(u):
-            gate[u] = ring.tile([P, width[units[u][0]]], F32, name="gate", align_bytes=64, bufs=4)
-            nc.scalar.activation(gate[u][:], diff[u][:], ACT.Tanh)
+        def apply_tanh(half, t):
+            gate[half, t] = passing("gate")
+            nc.scalar.activation(gate[half, t][:], difference[half, t][:], ACT.Tanh)
 
-        def scale(u):
-            c, t = units[u]
+        def make_z(half, t):
             nc.vector.scalar_tensor_tensor(
-                z_rows[c][:, t, :], y_ps[t][:, CHUNKS[c]], gain[:, t : t + 1], gate[u][:], ALU.mult, ALU.mult
+                z_rows[half][:, t, :], y_psum[t][:, HALVES[half]], gain[:, t : t + 1], gate[half, t][:],
+                ALU.mult, ALU.mult,
             )
 
-        def group(u):
-            c, t = units[u]
+        def group_z(half, t):
             if t == PACK - 1:
-                interleave(nc.scalar.copy if c in (0,) else nc.vector.tensor_copy, z_grouped[c], z_rows[c])
+                group(half, z_grouped[half], z_rows[half])
 
-        def project(u):
-            c, t = units[u]
+        def make_h(half, t):
             if t == PACK - 1:
-                z_words = sb(f"z_words{c}", [P, width[c]], U32)
-                z_plane = sb(f"z_plane{c}", [P, width[c]], U8)
-                nc.vector.quantize_mx(
-                    out=z_words[:].bitcast(FP8X4), scales=z_plane[:],
-                    in_=z_grouped[c][:].rearrange("p j t -> p (j t)"),
-                )
+                z_words = sb(f"z_words{half}", [P, HALF], U32)
+                z_plane = sb(f"z_plane{half}", [P, HALF], U8)
+                quantise(z_words[:], z_plane[:], z_grouped[half])
                 for m in range(PACK):
-                    if c in {1: slice(0, 256)}:
-                        move(m in (), h_sb[m][:, {1: slice(0, 256)}[c]], h_ps[m][:, {1: slice(0, 256)}[c]])
-                    product(h_ps[m][:, CHUNKS[c]], w3, w3s, 4, m, z_words[:], z_plane[:])
+                    if half == 1:
+                        move(False, h[m][:, HALVES[0]], h_psum[m][:, HALVES[0]])
+                    product(h_psum[m][:, HALVES[half]], w3, w3_plane, m, z_words[:], z_plane[:])
 
-        stages = [fetch, squash, scale, group, project]
-        for step in range(len(units) + len(stages) - 1):
-            for lag, stage in enumerate(stages):
-                if 0 <= step - lag < len(units):
-                    stage(step - lag)
+        pipeline([subtract_d, apply_tanh, make_z, group_z, make_h])
 
-
-        halves = [slice(0, HALF), slice(HALF, S)]
         st = [sb(f"st{t}", [P, S], F32) for t in range(PACK)]
-        near = [sb(f"near{t}", [P, S], F32) for t in range(PACK)]
-        last = slice(256, 512)
+        h_at_n3 = [sb(f"h_at_n3{t}", [P, S], F32) for t in range(PACK)]
         for t in range(PACK):
-            move(t in (0, 2), h_sb[t][:, last], h_ps[t][:, last])
-            for i, cols in enumerate(halves):
-                move(t in (0, 2) or (t, i) in (0, 2), near[t][:, cols], h_sb[t][:].indirect(part(n3_t, cols)))
-        owidth = [cols.stop - cols.start for cols in OCHUNKS]
-        res = [sb(f"res{c}", [P, PACK, w], F32) for c, w in enumerate(owidth)]
+            move(t % 2 == 0, h[t][:, HALVES[1]], h_psum[t][:, HALVES[1]])
+            for half, cols in enumerate(HALVES):
+                move(t % 2 == 0, h_at_n3[t][:, cols], look_up(h[t], n3_list, half))
+        for t in range(PACK):
+            nc.vector.tensor_tensor(st[t][:], h_psum[t][:], h_at_n3[t][:], ALU.subtract)
+        minus_half_st = sb("minus_half_st", [P, S], F32)
+        nc.vector.tensor_scalar(minus_half_st[:], st[FUSED_TILE][:], -0.5, None, ALU.mult)
+
+        result = [sb(f"result{half}", [P, PACK, HALF], F32) for half in range(2)]
+        out_grouped = [sb(f"out_grouped{half}", [P, HALF, PACK], BF16) for half in range(2)]
+        out_words = sb("out_words", [P, S], U32)
+        out_plane = sb("out_plane", [P, S], U8)
         out_rows = out_0.rearrange("(p t) j -> p t j", t=PACK)
-        minus_half = {}
-        for t in (0, 1, 2, 3):
-            nc.vector.tensor_tensor(st[t][:], h_ps[t][:], near[t][:], ALU.subtract)
-        for t in (0,):
-            minus_half[t] = sb(f"minus_half{t}", [P, S], F32)
-            nc.vector.tensor_scalar(minus_half[t][:], st[t][:], -0.5, None, ALU.mult)
+        out_codes = out_1[0].rearrange("p n r -> p (n r)").bitcast(I32)
 
-        o_words = sb("o_words", [P, S], U32)
-        o_plane = sb("o_plane", [P, S], U8)
-        words_out = out_1[0].rearrange("p n r -> p (n r)").bitcast(I32)
-        o_grouped = [sb(f"o_grouped{c}", [P, w, PACK], BF16) for c, w in enumerate(owidth)]
-        units2 = [(c, t) for c in range(len(OCHUNKS)) for t in (0, 1, 2, 3)]
-
-        def finish(u):
-            c, t = units2[u]
-            cols = OCHUNKS[c]
-            if t in (0,):
-                nc.vector.tensor_tensor(res[c][:, t, :], minus_half[t][:].indirect(part(n3_t, cols)), st[t][:, cols], ALU.add)
-            else:
-                far = ring.tile([P, owidth[c]], F32, name="far", align_bytes=64, bufs=4)
-                move((c, t) in (), far[:], st[t][:].indirect(part(n3_t, cols)))
-                nc.vector.scalar_tensor_tensor(res[c][:, t, :], far[:], -0.5, st[t][:, cols], ALU.mult, ALU.add)
-            if t % 2 == 2 - 1:
-                nc.sync.dma_start(out_rows[:, t + 1 - 2 : t + 1, cols], res[c][:, t + 1 - 2 : t + 1, :])
-
-        def regroup(u):
-            c, t = units2[u]
-            if t == (0, 1, 2, 3)[-1]:
-                interleave(nc.scalar.copy if c in (0,) else nc.vector.tensor_copy, o_grouped[c], res[c])
-
-        def pack(u):
-            c, t = units2[u]
-            cols = OCHUNKS[c]
-            if t == (0, 1, 2, 3)[-1]:
-                nc.vector.quantize_mx(
-                    out=o_words[:, cols].bitcast(FP8X4), scales=o_plane[:, cols],
-                    in_=o_grouped[c][:].rearrange("p j t -> p (j t)"),
+        def make_out(half, t):
+            cols = HALVES[half]
+            if t == FUSED_TILE:
+                nc.vector.tensor_tensor(
+                    result[half][:, t, :], look_up(minus_half_st, n3_list, half), st[t][:, cols], ALU.add
                 )
-                nc.sync.dma_start(words_out[:, cols], o_words[:, cols].bitcast(I32))
+            else:
+                st_at_n3 = passing("st_at_n3")
+                move(False, st_at_n3[:], look_up(st[t], n3_list, half))
+                nc.vector.scalar_tensor_tensor(
+                    result[half][:, t, :], st_at_n3[:], -0.5, st[t][:, cols], ALU.mult, ALU.add
+                )
+            if t % 2 == 1:
+                nc.sync.dma_start(out_rows[:, t - 1 : t + 1, cols], result[half][:, t - 1 : t + 1, :])
 
-        stages2 = [finish, regroup, pack]
-        for step in range(len(units2) + len(stages2) - 1):
-            for lag, stage in enumerate(stages2):
-                if 0 <= step - lag < len(units2):
-                    stage(step - lag)
+        def group_out(half, t):
+            if t == PACK - 1:
+                group(half, out_grouped[half], result[half])
+
+        def quantise_out(half, t):
+            if t == PACK - 1:
+                cols = HALVES[half]
+                quantise(out_words[:, cols], out_plane[:, cols], out_grouped[half])
+                nc.sync.dma_start(out_codes[:, cols], out_words[:, cols].bitcast(I32))
+
+        pipeline([make_out, group_out, quantise_out])
+
         for q in range(4):
-            (nc.sync if q == 3 else nc.scalar).dma_start(out_2[0, 4 * q : 4 * q + 4, :].bitcast(I32), o_plane[32 * q : 32 * q + 4, :].bitcast(I32))
+            queue = nc.sync if q == 3 else nc.scalar
+            queue.dma_start(
+                out_2[0, PACK * q : PACK * (q + 1), :].bitcast(I32), out_plane[32 * q : 32 * q + PACK, :].bitcast(I32)
+            )

from contextlib import ExitStack

import concourse.mybir as mybir

F32 = mybir.dt.float32
BF16 = mybir.dt.bfloat16
I32 = mybir.dt.int32
U32 = mybir.dt.uint32
U16 = mybir.dt.uint16
U8 = mybir.dt.uint8
FP8X4 = mybir.dt.float8_e4m3fn_x4
ALU = mybir.AluOpType
ACT = mybir.ActivationFunctionType

P = 128
T = 2048
S = 512
PACK = 4
HALF = S // 2
HALVES = [slice(0, HALF), slice(HALF, S)]
RING = 4

FUSED_TILE = 0

FLOPS = 3 * 2 * S * S * S


def tile_picked_twhjointbtwice_none_po_kernel(
    tc, x_words, x_scales, w1_words, w1_scales, w2_words, w2_scales, gn, w3_words, w3_scales,
    offs, hz, n1, n2, n3, out_0, out_1, out_2,
):
    nc = tc.nc
    with ExitStack() as ctx:
        lists = ctx.enter_context(tc.tile_pool(name="lists", bufs=1))
        keep = ctx.enter_context(tc.tile_pool(name="keep", bufs=1))
        ring = ctx.enter_context(tc.tile_pool(name="ring", bufs=RING))
        psum = ctx.enter_context(tc.psum_pool(name="psum", bufs=1))

        def sb(name, shape, dtype):
            return keep.tile(shape, dtype, name=name, align_bytes=64)

        def passing(name):
            return ring.tile([P, HALF], F32, name=name, align_bytes=64)

        def zeroed(name, width):
            tile = sb(name, [P, width], U8)
            nc.vector.memset(tile[:].bitcast(I32), 0)
            return tile

        def load_list(name, src):
            tile = lists.tile([P, S // 16], U16, name=name)
            nc.sync.dma_start(tile[:], src)
            return tile

        def load_words(name, src, width):
            tile = sb(name, [P, width], I32)
            nc.sync.dma_start(tile[:], src[0].rearrange("p n r -> p (n r)").bitcast(I32))
            return tile

        def load_plane(plane, src):
            for q in range(4):
                rows = slice(32 * q, 32 * q + PACK)
                nc.sync.dma_start(plane[rows, :].bitcast(I32), src[0, PACK * q : PACK * (q + 1), :].bitcast(I32))

        def deal_words(copy, name, raw):
            dealt = sb(name, [P, PACK, P], U32)
            copy(
                dealt[:].rearrange("p t (c i) -> p c t i", i=4),
                raw[:].bitcast(U32).rearrange("p (c i t) -> p c t i", i=4, t=PACK),
            )
            return dealt

        def deal_plane(name, raw):
            dealt = sb(name, [P, PACK, P], U8)
            nc.vector.tensor_copy(dealt[:], raw[:].rearrange("p (m t) -> p t m", t=PACK))
            return dealt

        def gather_packed(name, window, dtype, offsets):
            picked = sb(name, [P, S], dtype)
            nc.vector.tensor_copy(picked[:], window[:].bitcast(dtype).indirect(offsets[:]))
            return picked

        def place_rows(plane, picked):
            for r in range(PACK):
                nc.sync.dma_start(plane[r:P:32, :].bitcast(I32), picked[8 * r : P : 32, :].bitcast(I32))

        def product(out, weights, weight_plane, t, words, plane):
            nc.tensor.matmul_mx(
                out=out, lhsT=weights[:, t, :].bitcast(FP8X4), lhsT_scale=weight_plane[:, t, :],
                rhs=words.bitcast(FP8X4), rhs_scale=plane, start=True, stop=True,
            )

        def move(on_vector, out, in_):
            if on_vector:
                nc.vector.tensor_copy(out, in_)
            else:
                nc.scalar.activation(out, in_, ACT.Copy)

        def look_up(window, offsets, half):
            return window[:].indirect(offsets[:, half * HALF // 16 : (half + 1) * HALF // 16])

        def group(half, grouped, rows):
            copy = nc.vector.tensor_copy if half else nc.scalar.copy
            copy(grouped[:].rearrange("p (c i) t -> p c t i", i=4), rows[:].rearrange("p t (c i) -> p c t i", i=4))

        def quantise(words, plane, grouped):
            nc.vector.quantize_mx(out=words.bitcast(FP8X4), scales=plane, in_=grouped[:].rearrange("p j t -> p (j t)"))

        def pipeline(stages):
            pieces = [(half, t) for half in range(2) for t in range(PACK)]
            for step in range(len(pieces) + len(stages) - 1):
                for lag, stage in enumerate(stages):
                    if 0 <= step - lag < len(pieces):
                        stage(*pieces[step - lag])

        w2_plane_raw = zeroed("w2_plane_raw", S)
        x_rows = zeroed("x_rows", T)
        hz_plane = zeroed("hz_plane", S)
        w1_plane_raw = zeroed("w1_plane_raw", S)
        offs_plane = zeroed("offs_plane", S)

        hz_list = load_list("hz_list", hz)
        offs_list = load_list("offs_list", offs)
        load_plane(w2_plane_raw, w2_scales)
        nc.sync.dma_start(x_rows[0:P:8, :].bitcast(I32), x_scales[0].bitcast(I32))
        x_table = load_words("x_table", x_words, T)
        w2_raw = load_words("w2_raw", w2_words, S)

        w2_plane = deal_plane("w2_plane", w2_plane_raw)
        hz_rows = gather_packed("hz_rows", x_rows, U8, hz_list)
        place_rows(hz_plane, hz_rows)
        hz_words = gather_packed("hz_words", x_table, U32, hz_list)
        offs_rows = gather_packed("offs_rows", x_rows, U8, offs_list)
        offs_words = gather_packed("offs_words", x_table, U32, offs_list)
        w2 = deal_words(nc.scalar.copy, "w2", w2_raw)

        n2_list = load_list("n2_list", n2)
        w1_raw = load_words("w1_raw", w1_words, S)
        load_plane(w1_plane_raw, w1_scales)
        place_rows(offs_plane, offs_rows)
        n1_list = load_list("n1_list", n1)
        gain = sb("gain", [P, PACK], F32)
        nc.sync.dma_start(gain[:], gn.rearrange("(p t) o -> p (t o)", t=PACK))
        w3_raw = load_words("w3_raw", w3_words, S)
        w3_plane_raw = zeroed("w3_plane_raw", S)
        load_plane(w3_plane_raw, w3_scales)
        n3_list = load_list("n3_list", n3)
        w1 = deal_words(nc.scalar.copy, "w1", w1_raw)
        w1_plane = deal_plane("w1_plane", w1_plane_raw)
        w3_plane = deal_plane("w3_plane", w3_plane_raw)
        w3 = deal_words(nc.vector.tensor_copy, "w3", w3_raw)

        d_psum = [psum.tile([P, S], F32, name=f"d_psum{t}", tag=f"bank{t}") for t in range(PACK)]
        y_psum = [psum.tile([P, S], F32, name=f"y_psum{t}", tag=f"bank{PACK + t}") for t in range(PACK)]
        for t in range(PACK):
            product(d_psum[t][:], w2, w2_plane, t, hz_words[:], hz_plane[:])
        for t in range(PACK):
            product(y_psum[t][:], w1, w1_plane, t, offs_words[:], offs_plane[:])

        d = [sb(f"d{t}", [P, S], F32) for t in range(PACK)]
        h = [sb(f"h{t}", [P, S], F32) for t in range(PACK)]
        h_psum = [psum.tile([P, S], F32, name=f"h_psum{t}", tag=f"bank{t}") for t in range(PACK)]
        z_rows = [sb(f"z_rows{half}", [P, PACK, HALF], BF16) for half in range(2)]
        z_grouped = [sb(f"z_grouped{half}", [P, HALF, PACK], BF16) for half in range(2)]
        difference, gate = {}, {}

        def subtract_d(half, t):
            if half == 0:
                move(t > 0, d[t][:], d_psum[t][:])
            d_at_n2 = passing("d_at_n2")
            difference[half, t] = passing("difference")
            move(False, d_at_n2[:], look_up(d[t], n2_list, half))
            nc.vector.tensor_tensor(difference[half, t][:], look_up(d[t], n1_list, half), d_at_n2[:], ALU.subtract)

        def apply_tanh(half, t):
            gate[half, t] = passing("gate")
            nc.scalar.activation(gate[half, t][:], difference[half, t][:], ACT.Tanh)

        def make_z(half, t):
            nc.vector.scalar_tensor_tensor(
                z_rows[half][:, t, :], y_psum[t][:, HALVES[half]], gain[:, t : t + 1], gate[half, t][:],
                ALU.mult, ALU.mult,
            )

        def group_z(half, t):
            if t == PACK - 1:
                group(half, z_grouped[half], z_rows[half])

        def make_h(half, t):
            if t == PACK - 1:
                z_words = sb(f"z_words{half}", [P, HALF], U32)
                z_plane = sb(f"z_plane{half}", [P, HALF], U8)
                quantise(z_words[:], z_plane[:], z_grouped[half])
                for m in range(PACK):
                    if half == 1:
                        move(False, h[m][:, HALVES[0]], h_psum[m][:, HALVES[0]])
                    product(h_psum[m][:, HALVES[half]], w3, w3_plane, m, z_words[:], z_plane[:])

        pipeline([subtract_d, apply_tanh, make_z, group_z, make_h])

        st = [sb(f"st{t}", [P, S], F32) for t in range(PACK)]
        h_at_n3 = [sb(f"h_at_n3{t}", [P, S], F32) for t in range(PACK)]
        for t in range(PACK):
            move(t % 2 == 0, h[t][:, HALVES[1]], h_psum[t][:, HALVES[1]])
            for half, cols in enumerate(HALVES):
                move(t % 2 == 0, h_at_n3[t][:, cols], look_up(h[t], n3_list, half))
        for t in range(PACK):
            nc.vector.tensor_tensor(st[t][:], h_psum[t][:], h_at_n3[t][:], ALU.subtract)
        minus_half_st = sb("minus_half_st", [P, S], F32)
        nc.vector.tensor_scalar(minus_half_st[:], st[FUSED_TILE][:], -0.5, None, ALU.mult)

        result = [sb(f"result{half}", [P, PACK, HALF], F32) for half in range(2)]
        out_grouped = [sb(f"out_grouped{half}", [P, HALF, PACK], BF16) for half in range(2)]
        out_words = sb("out_words", [P, S], U32)
        out_plane = sb("out_plane", [P, S], U8)
        out_rows = out_0.rearrange("(p t) j -> p t j", t=PACK)
        out_codes = out_1[0].rearrange("p n r -> p (n r)").bitcast(I32)

        def make_out(half, t):
            cols = HALVES[half]
            if t == FUSED_TILE:
                nc.vector.tensor_tensor(
                    result[half][:, t, :], look_up(minus_half_st, n3_list, half), st[t][:, cols], ALU.add
                )
            else:
                st_at_n3 = passing("st_at_n3")
                move(False, st_at_n3[:], look_up(st[t], n3_list, half))
                nc.vector.scalar_tensor_tensor(
                    result[half][:, t, :], st_at_n3[:], -0.5, st[t][:, cols], ALU.mult, ALU.add
                )
            if t % 2 == 1:
                nc.sync.dma_start(out_rows[:, t - 1 : t + 1, cols], result[half][:, t - 1 : t + 1, :])

        def group_out(half, t):
            if t == PACK - 1:
                group(half, out_grouped[half], result[half])

        def quantise_out(half, t):
            if t == PACK - 1:
                cols = HALVES[half]
                quantise(out_words[:, cols], out_plane[:, cols], out_grouped[half])
                nc.sync.dma_start(out_codes[:, cols], out_words[:, cols].bitcast(I32))

        pipeline([make_out, group_out, quantise_out])

        for q in range(4):
            queue = nc.sync if q == 3 else nc.scalar
            queue.dma_start(
                out_2[0, PACK * q : PACK * (q + 1), :].bitcast(I32), out_plane[32 * q : 32 * q + PACK, :].bitcast(I32)
            )
